import numpy as np, ml_dtypes
CORES = [2,42,66,74,82,90,114]
N = 7
import mx_ref
NC = 256
SEQ = [0,0,0,0,1,2,2]
WID = [176,230,172,128,130,256,200]
BF = ml_dtypes.bfloat16
def setup_inputs(rng):
    def f(*shape):
        return mx_ref.flush((rng.standard_normal(shape, dtype=np.float32) * np.exp2(rng.integers(-2, 3, shape[:-1] + (1,)))).astype(BF))
    return {"w": f(N, 128, 512), "x": f(N, 128, 4 * NC)}
def setup_inputs_blocks(rng):
    d = setup_inputs(rng)
    for k in ("w", "x"): d[k] = mx_ref.spread(d[k], rng, 4)
    return d
def setup_inputs_wide(rng):
    d = setup_inputs(rng)
    for k in ("w", "x"): d[k] = mx_ref.flush((d[k].astype(np.float32) * np.exp2(rng.integers(-10, 11, (N, 1, 1))).astype(np.float32)).astype(BF))
    return d
def reference(w, x):
    y = np.full((N, 128, 706), np.nan, np.float32)
    for r in range(N):
        qw = mx_ref.quantize(w[r]); a = 0
        for j in range(N):
            if SEQ[j] == SEQ[r]:
                y[r][:, a:a + WID[j]] = mx_ref.matmul(qw, mx_ref.quantize(x[j][:, :4 * WID[j]])); a += WID[j]
    return {"y": y}

@@ -1,0 +1,137 @@
+from concourse.bass import DstId, RemoteDMATransfer
+from concourse.mybir import dt, ActivationFunctionType
+
+SLOT = 256
+MAXM = 4
+YC = 706
+
+SCRATCH = {
+    "xb": ("sbuf", [128, 4 * SLOT], "bfloat16"),
+    "wb": ("sbuf", [128, 512], "bfloat16"),
+    "xq": ("sbuf", [128, MAXM * SLOT], "float8_e4m3fn_x4"),
+    "xs": ("sbuf", [128, MAXM * SLOT], "uint8"),
+    "wq": ("sbuf", [128, 128], "float8_e4m3fn_x4"),
+    "ws": ("sbuf", [128, 128], "uint8"),
+    "ps": ("psum", [128, 512 * MAXM], "float32"),
+    "yb": ("sbuf", [128, YC], "float32"),
+}
+SEMAPHORES = (["sx", "sw", "qx", "qw", "sent", "sta", "stb"]
+              + ["arr%d" % k for k in range(MAXM)]
+              + ["mm%d" % k for k in range(MAXM)]
+              + ["cp%d" % k for k in range(MAXM)])
+
+
+def _hops(topo, a, b):
+    ca, cb = topo.chip(a), topo.chip(b)
+    if ca == cb:
+        return 0
+    return 1 if (topo.mates(ca, cb) or topo.same_plane(ca, cb)) else 2
+
+
+def _perms(items):
+    if not items:
+        return [[]]
+    out = []
+    for i in range(len(items)):
+        for rest in _perms(items[:i] + items[i + 1:]):
+            out.append([items[i]] + rest)
+    return out
+
+
+def _rounds(topo, cores):
+    m = len(cores)
+    used, rounds = set(), []
+    perms = _perms(list(range(m)))
+    for _ in range(m - 1):
+        best, score = None, -1
+        for p in perms:
+            if any(p[i] == i or (i, p[i]) in used for i in range(m)):
+                continue
+            s = sum(_hops(topo, cores[i], cores[p[i]]) for i in range(m))
+            if s > score:
+                best, score = p, s
+        rounds.append(best)
+        used |= set((i, best[i]) for i in range(m))
+    return rounds
+
+
+def _mask(topo, src, dsts):
+    m = topo.mask(src, dsts[0])
+    for d in dsts[1:]:
+        m &= topo.mask(src, d)
+    return m, bin(m).count("1")
+
+
+def rank_program(g, core, T, topo):
+    r = T.rank_of(core)
+    if r is None:
+        return
+    SEQ, WID = T.tables["SEQ"], T.tables["WID"]
+    sem = T.sem
+    mem = [j for j in range(len(SEQ)) if SEQ[j] == SEQ[r]]
+    cores = [T.cores[j] for j in mem]
+    m, me = len(mem), mem.index(r)
+    wid = [WID[j] for j in mem]
+    yoff = [sum(wid[:k]) for k in range(m)]
+    rounds = _rounds(topo, cores)
+    dests = [[rd[i] for rd in rounds] for i in range(m)]
+
+    def codes(k):
+        return T.xq[:, k * SLOT:k * SLOT + wid[k]]
+
+    def plane(k):
+        return T.xs[:, k * SLOT:k * SLOT + wid[k]]
+
+    W = wid[me]
+    g.sync.dma_start(T.xb[:, :4 * W], T.x[:, :4 * W]).then_inc(sem.sx, 16)
+    g.sync.dma_start(T.wb[:], T.w[:]).then_inc(sem.sw, 16)
+
+    g.vector.wait_ge(sem.sx, 16)
+    g.vector.quantize_mx(codes(me), plane(me), T.xb[:, :4 * W]).then_inc(sem.qx, 1)
+    g.vector.wait_ge(sem.sw, 16)
+    g.vector.quantize_mx(T.wq[:], T.ws[:], T.wb[:]).then_inc(sem.qw, 1)
+
+    left = 0
+    if m > 1:
+        to = [cores[k] for k in dests[me]]
+        mask, ne = _mask(topo, core, to)
+        ids = [DstId(rid=topo.addr(c)[0], pnc=topo.addr(c)[1]) for c in to]
+        g.wait_ge(sem.qx, 1)
+        g.remote_dma_fused([RemoteDMATransfer(
+            dst_ids=ids, dma_engine_mask=mask, remote_sem=sem["arr%d" % me],
+            srcs=[codes(me).bitcast(dt.uint8)], dsts=[codes(me).bitcast(dt.uint8) for _ in to])], local_sem=sem.sent)
+        g.remote_dma_fused([RemoteDMATransfer(
+            dst_ids=ids, dma_engine_mask=mask, remote_sem=sem["arr%d" % me],
+            srcs=[plane(me)], dsts=[plane(me) for _ in to])], local_sem=sem.sent)
+        left = 2 * ne
+
+    order = [me] + sorted((k for k in range(m) if k != me), key=lambda k: (wid[k], dests[k].index(me)))
+    g.tensor.wait_ge(sem.qx, 1)
+    g.tensor.wait_ge(sem.qw, 1)
+    for n, k in enumerate(order):
+        if k != me:
+            ne_k = _mask(topo, cores[k], [cores[d] for d in dests[k]])[1]
+            g.tensor.wait_ge(sem["arr%d" % k], 2 * ne_k)
+        g.tensor.matmul_mx(T.ps[:, 512 * n:512 * n + wid[k]], T.wq[:], T.ws[:], codes(k), plane(k),
+                           True, True).then_inc(sem["mm%d" % n], 1)
+
+    stored = [0, 0]
+    for n, k in enumerate(order):
+        odd = n % 2
+        a, b = yoff[k], yoff[k] + wid[k]
+        src = T.ps[:, 512 * n:512 * n + wid[k]]
+        if odd:
+            g.scalar.wait_ge(sem["mm%d" % n], 1)
+            g.scalar.activation(T.yb[:, a:b], src, ActivationFunctionType.Copy).then_inc(sem["cp%d" % n], 1)
+        else:
+            g.vector.wait_ge(sem["mm%d" % n], 1)
+            g.vector.tensor_copy(T.yb[:, a:b], src).then_inc(sem["cp%d" % n], 1)
+        q = g.scalar if odd else g.sync
+        if left and not stored[odd]:
+            q.wait_ge(sem.sent, left)
+        q.wait_ge(sem["cp%d" % n], 1)
+        q.dma_start(T.y[:, a:b], T.yb[:, a:b]).then_inc(sem.stb if odd else sem.sta, 16)
+        stored[odd] += 16
+    g.sync.wait_ge(sem.sta, stored[0])
+    if stored[1]:
+        g.scalar.wait_ge(sem.stb, stored[1])

@@ -4,6 +4,7 @@ from concourse.mybir import dt, ActivationFunctionType
 SLOT = 256
 MAXM = 4
 YC = 706
+NCORES = 128
 
 SCRATCH = {
     "xb": ("sbuf", [128, 4 * SLOT], "bfloat16"),
@@ -15,7 +16,7 @@ SCRATCH = {
     "ps": ("psum", [128, 512 * MAXM], "float32"),
     "yb": ("sbuf", [128, YC], "float32"),
 }
-SEMAPHORES = (["sx", "sw", "qx", "qw", "sent", "sta", "stb"]
+SEMAPHORES = (["sx", "sw", "qx", "qw", "sent", "sta", "stb", "hp", "hs"]
               + ["arr%d" % k for k in range(MAXM)]
               + ["mm%d" % k for k in range(MAXM)]
               + ["cp%d" % k for k in range(MAXM)])
@@ -62,19 +63,75 @@ def _mask(topo, src, dsts):
     return m, bin(m).count("1")
 
 
+def _ids(topo, cs):
+    return [DstId(rid=topo.addr(c)[0], pnc=topo.addr(c)[1]) for c in cs]
+
+
+def _pick(T, topo, src, dsts, taken):
+    best, key = None, None
+    for c in range(NCORES):
+        if topo.chip(c) != topo.chip(src) or c in T.cores or c in taken:
+            continue
+        if not all(topo.may_write(c, d) for d in dsts):
+            continue
+        k = (topo.die(c) == topo.die(src), sum(1 for d in T.cores if topo.may_write(c, d)), c)
+        if key is None or k < key:
+            best, key = c, k
+    return best
+
+
+def _plan(T, topo, s):
+    SEQ = T.tables["SEQ"]
+    mem = [j for j in range(len(SEQ)) if SEQ[j] == s]
+    cores = [T.cores[j] for j in mem]
+    m = len(mem)
+    rounds = _rounds(topo, cores)
+    dests = [[rd[i] for rd in rounds] for i in range(m)]
+    carriers = []
+    for i in range(m):
+        jobs = [dests[i][:-1], dests[i][-1:]] if m > 2 else []
+        got, taken = [], []
+        for job in jobs:
+            h = _pick(T, topo, cores[i], [cores[k] for k in job], taken)
+            if h is None:
+                break
+            got.append((h, job))
+            taken.append(h)
+        if not jobs or len(got) < len(jobs):
+            got = [(cores[i], dests[i])] if m > 1 else []
+        carriers.append(got)
+    return mem, cores, dests, carriers
+
+
 def rank_program(g, core, T, topo):
-    r = T.rank_of(core)
-    if r is None:
-        return
     SEQ, WID = T.tables["SEQ"], T.tables["WID"]
     sem = T.sem
-    mem = [j for j in range(len(SEQ)) if SEQ[j] == SEQ[r]]
-    cores = [T.cores[j] for j in mem]
+    r = T.rank_of(core)
+
+    if r is None:
+        for s in sorted(set(SEQ)):
+            mem, cores, dests, carriers = _plan(T, topo, s)
+            for i in range(len(mem)):
+                for h, job in carriers[i]:
+                    if h != core:
+                        continue
+                    hs = [c for c, _ in carriers[i]]
+                    off = _mask(topo, cores[i], [cores[k] for k in dests[i]])[0]
+                    n_in = bin(_mask(topo, cores[i], hs)[0] & ~off).count("1")
+                    pl = T.xs[:, i * SLOT:i * SLOT + WID[mem[i]]]
+                    to = [cores[k] for k in job]
+                    mask, ne = _mask(topo, core, to)
+                    g.wait_ge(sem.hp, n_in)
+                    g.remote_dma_fused([RemoteDMATransfer(
+                        dst_ids=_ids(topo, to), dma_engine_mask=mask, remote_sem=sem["arr%d" % i],
+                        srcs=[pl], dsts=[pl for _ in to])], local_sem=sem.hs)
+                    g.wait_ge(sem.hs, ne)
+        return
+
+    mem, cores, dests, carriers = _plan(T, topo, SEQ[r])
     m, me = len(mem), mem.index(r)
     wid = [WID[j] for j in mem]
     yoff = [sum(wid[:k]) for k in range(m)]
-    rounds = _rounds(topo, cores)
-    dests = [[rd[i] for rd in rounds] for i in range(m)]
 
     def codes(k):
         return T.xq[:, k * SLOT:k * SLOT + wid[k]]
@@ -95,23 +152,33 @@ def rank_program(g, core, T, topo):
     if m > 1:
         to = [cores[k] for k in dests[me]]
         mask, ne = _mask(topo, core, to)
-        ids = [DstId(rid=topo.addr(c)[0], pnc=topo.addr(c)[1]) for c in to]
+        helped = carriers[me][0][0] != core
         g.wait_ge(sem.qx, 1)
+        if helped:
+            hs = [c for c, _ in carriers[me]]
+            hmask = _mask(topo, core, hs)[0] & ~mask
+            g.remote_dma_fused([RemoteDMATransfer(
+                dst_ids=_ids(topo, hs), dma_engine_mask=hmask, remote_sem=sem.hp,
+                srcs=[plane(me)], dsts=[plane(me) for _ in hs])], local_sem=sem.sent)
+            left += bin(hmask).count("1")
         g.remote_dma_fused([RemoteDMATransfer(
-            dst_ids=ids, dma_engine_mask=mask, remote_sem=sem["arr%d" % me],
+            dst_ids=_ids(topo, to), dma_engine_mask=mask, remote_sem=sem["arr%d" % me],
             srcs=[codes(me).bitcast(dt.uint8)], dsts=[codes(me).bitcast(dt.uint8) for _ in to])], local_sem=sem.sent)
-        g.remote_dma_fused([RemoteDMATransfer(
-            dst_ids=ids, dma_engine_mask=mask, remote_sem=sem["arr%d" % me],
-            srcs=[plane(me)], dsts=[plane(me) for _ in to])], local_sem=sem.sent)
-        left = 2 * ne
+        left += ne
+        if not helped:
+            g.remote_dma_fused([RemoteDMATransfer(
+                dst_ids=_ids(topo, to), dma_engine_mask=mask, remote_sem=sem["arr%d" % me],
+                srcs=[plane(me)], dsts=[plane(me) for _ in to])], local_sem=sem.sent)
+            left += ne
 
     order = [me] + sorted((k for k in range(m) if k != me), key=lambda k: (wid[k], dests[k].index(me)))
     g.tensor.wait_ge(sem.qx, 1)
     g.tensor.wait_ge(sem.qw, 1)
     for n, k in enumerate(order):
         if k != me:
-            ne_k = _mask(topo, cores[k], [cores[d] for d in dests[k]])[1]
-            g.tensor.wait_ge(sem["arr%d" % k], 2 * ne_k)
+            n_codes = _mask(topo, cores[k], [cores[d] for d in dests[k]])[1]
+            n_plane = [_mask(topo, c, [cores[d] for d in job])[1] for c, job in carriers[k] if me in job][0]
+            g.tensor.wait_ge(sem["arr%d" % k], n_codes + n_plane)
         g.tensor.matmul_mx(T.ps[:, 512 * n:512 * n + wid[k]], T.wq[:], T.ws[:], codes(k), plane(k),
                            True, True).then_inc(sem["mm%d" % n], 1)
 

from concourse.bass import DstId, RemoteDMATransfer
from concourse.mybir import dt, ActivationFunctionType

SLOT = 256
MAXM = 4
YC = 706
NCORES = 128

SCRATCH = {
    "xb": ("sbuf", [128, 4 * SLOT], "bfloat16"),
    "wb": ("sbuf", [128, 512], "bfloat16"),
    "xq": ("sbuf", [128, MAXM * SLOT], "float8_e4m3fn_x4"),
    "xs": ("sbuf", [128, MAXM * SLOT], "uint8"),
    "wq": ("sbuf", [128, 128], "float8_e4m3fn_x4"),
    "ws": ("sbuf", [128, 128], "uint8"),
    "ps": ("psum", [128, 512 * MAXM], "float32"),
    "yb": ("sbuf", [128, YC], "float32"),
}
SEMAPHORES = (["sx", "sw", "qx", "qw", "sent", "sta", "stb", "hp", "hs"]
              + ["arr%d" % k for k in range(MAXM)]
              + ["mm%d" % k for k in range(MAXM)]
              + ["cp%d" % k for k in range(MAXM)])


def _hops(topo, a, b):
    ca, cb = topo.chip(a), topo.chip(b)
    if ca == cb:
        return 0
    return 1 if (topo.mates(ca, cb) or topo.same_plane(ca, cb)) else 2


def _perms(items):
    if not items:
        return [[]]
    out = []
    for i in range(len(items)):
        for rest in _perms(items[:i] + items[i + 1:]):
            out.append([items[i]] + rest)
    return out


def _rounds(topo, cores):
    m = len(cores)
    used, rounds = set(), []
    perms = _perms(list(range(m)))
    for _ in range(m - 1):
        best, score = None, -1
        for p in perms:
            if any(p[i] == i or (i, p[i]) in used for i in range(m)):
                continue
            s = sum(_hops(topo, cores[i], cores[p[i]]) for i in range(m))
            if s > score:
                best, score = p, s
        rounds.append(best)
        used |= set((i, best[i]) for i in range(m))
    return rounds


def _mask(topo, src, dsts):
    m = topo.mask(src, dsts[0])
    for d in dsts[1:]:
        m &= topo.mask(src, d)
    return m, bin(m).count("1")


def _ids(topo, cs):
    return [DstId(rid=topo.addr(c)[0], pnc=topo.addr(c)[1]) for c in cs]


def _pick(T, topo, src, dsts, taken):
    best, key = None, None
    for c in range(NCORES):
        if topo.chip(c) != topo.chip(src) or c in T.cores or c in taken:
            continue
        if not all(topo.may_write(c, d) for d in dsts):
            continue
        k = (topo.die(c) == topo.die(src), sum(1 for d in T.cores if topo.may_write(c, d)), c)
        if key is None or k < key:
            best, key = c, k
    return best


def _plan(T, topo, s):
    SEQ = T.tables["SEQ"]
    mem = [j for j in range(len(SEQ)) if SEQ[j] == s]
    cores = [T.cores[j] for j in mem]
    m = len(mem)
    rounds = _rounds(topo, cores)
    dests = [[rd[i] for rd in rounds] for i in range(m)]
    carriers = []
    for i in range(m):
        jobs = [dests[i][:-1], dests[i][-1:]] if m > 2 else []
        got, taken = [], []
        for job in jobs:
            h = _pick(T, topo, cores[i], [cores[k] for k in job], taken)
            if h is None:
                break
            got.append((h, job))
            taken.append(h)
        if not jobs or len(got) < len(jobs):
            got = [(cores[i], dests[i])] if m > 1 else []
        carriers.append(got)
    return mem, cores, dests, carriers


def rank_program(g, core, T, topo):
    SEQ, WID = T.tables["SEQ"], T.tables["WID"]
    sem = T.sem
    r = T.rank_of(core)

    if r is None:
        for s in sorted(set(SEQ)):
            mem, cores, dests, carriers = _plan(T, topo, s)
            for i in range(len(mem)):
                for h, job in carriers[i]:
                    if h != core:
                        continue
                    hs = [c for c, _ in carriers[i]]
                    off = _mask(topo, cores[i], [cores[k] for k in dests[i]])[0]
                    n_in = bin(_mask(topo, cores[i], hs)[0] & ~off).count("1")
                    pl = T.xs[:, i * SLOT:i * SLOT + WID[mem[i]]]
                    to = [cores[k] for k in job]
                    mask, ne = _mask(topo, core, to)
                    g.wait_ge(sem.hp, n_in)
                    g.remote_dma_fused([RemoteDMATransfer(
                        dst_ids=_ids(topo, to), dma_engine_mask=mask, remote_sem=sem["arr%d" % i],
                        srcs=[pl], dsts=[pl for _ in to])], local_sem=sem.hs)
                    g.wait_ge(sem.hs, ne)
        return

    mem, cores, dests, carriers = _plan(T, topo, SEQ[r])
    m, me = len(mem), mem.index(r)
    wid = [WID[j] for j in mem]
    yoff = [sum(wid[:k]) for k in range(m)]

    def codes(k):
        return T.xq[:, k * SLOT:k * SLOT + wid[k]]

    def plane(k):
        return T.xs[:, k * SLOT:k * SLOT + wid[k]]

    W = wid[me]
    g.sync.dma_start(T.xb[:, :4 * W], T.x[:, :4 * W]).then_inc(sem.sx, 16)
    g.sync.dma_start(T.wb[:], T.w[:]).then_inc(sem.sw, 16)

    g.vector.wait_ge(sem.sx, 16)
    g.vector.quantize_mx(codes(me), plane(me), T.xb[:, :4 * W]).then_inc(sem.qx, 1)
    g.vector.wait_ge(sem.sw, 16)
    g.vector.quantize_mx(T.wq[:], T.ws[:], T.wb[:]).then_inc(sem.qw, 1)

    left = 0
    if m > 1:
        to = [cores[k] for k in dests[me]]
        mask, ne = _mask(topo, core, to)
        helped = carriers[me][0][0] != core
        g.wait_ge(sem.qx, 1)
        if helped:
            hs = [c for c, _ in carriers[me]]
            hmask = _mask(topo, core, hs)[0] & ~mask
            g.remote_dma_fused([RemoteDMATransfer(
                dst_ids=_ids(topo, hs), dma_engine_mask=hmask, remote_sem=sem.hp,
                srcs=[plane(me)], dsts=[plane(me) for _ in hs])], local_sem=sem.sent)
            left += bin(hmask).count("1")
        g.remote_dma_fused([RemoteDMATransfer(
            dst_ids=_ids(topo, to), dma_engine_mask=mask, remote_sem=sem["arr%d" % me],
            srcs=[codes(me).bitcast(dt.uint8)], dsts=[codes(me).bitcast(dt.uint8) for _ in to])], local_sem=sem.sent)
        left += ne
        if not helped:
            g.remote_dma_fused([RemoteDMATransfer(
                dst_ids=_ids(topo, to), dma_engine_mask=mask, remote_sem=sem["arr%d" % me],
                srcs=[plane(me)], dsts=[plane(me) for _ in to])], local_sem=sem.sent)
            left += ne

    order = [me] + sorted((k for k in range(m) if k != me), key=lambda k: (wid[k], dests[k].index(me)))
    g.tensor.wait_ge(sem.qx, 1)
    g.tensor.wait_ge(sem.qw, 1)
    for n, k in enumerate(order):
        if k != me:
            n_codes = _mask(topo, cores[k], [cores[d] for d in dests[k]])[1]
            n_plane = [_mask(topo, c, [cores[d] for d in job])[1] for c, job in carriers[k] if me in job][0]
            g.tensor.wait_ge(sem["arr%d" % k], n_codes + n_plane)
        g.tensor.matmul_mx(T.ps[:, 512 * n:512 * n + wid[k]], T.wq[:], T.ws[:], codes(k), plane(k),
                           True, True).then_inc(sem["mm%d" % n], 1)

    stored = [0, 0]
    for n, k in enumerate(order):
        odd = n % 2
        a, b = yoff[k], yoff[k] + wid[k]
        src = T.ps[:, 512 * n:512 * n + wid[k]]
        if odd:
            g.scalar.wait_ge(sem["mm%d" % n], 1)
            g.scalar.activation(T.yb[:, a:b], src, ActivationFunctionType.Copy).then_inc(sem["cp%d" % n], 1)
        else:
            g.vector.wait_ge(sem["mm%d" % n], 1)
            g.vector.tensor_copy(T.yb[:, a:b], src).then_inc(sem["cp%d" % n], 1)
        q = g.scalar if odd else g.sync
        if left and not stored[odd]:
            q.wait_ge(sem.sent, left)
        q.wait_ge(sem["cp%d" % n], 1)
        q.dma_start(T.y[:, a:b], T.yb[:, a:b]).then_inc(sem.stb if odd else sem.sta, 16)
        stored[odd] += 16
    g.sync.wait_ge(sem.sta, stored[0])
    if stored[1]:
        g.scalar.wait_ge(sem.stb, stored[1])
